import numpy as np
CORES = [44,45,46,47,172,173,174,175,300,301,302,303,428,429,430,431]
N = 16
TK = 512
NT = N * TK
EPS = 0.01
def setup_inputs(rng):
    x = (rng.standard_normal((N, 128, TK), dtype=np.float32) * (0.5 + np.arange(N, dtype=np.float32).reshape(N, 1, 1) / N) + rng.standard_normal((N, 128, 1), dtype=np.float32))
    return {"x": x, "dy": (rng.standard_normal((N, 128, TK), dtype=np.float32) + 0.5 * x + rng.standard_normal((1, 128, 1), dtype=np.float32))}
def reference(x, dy):
    X = x.astype(np.float64)
    mu = X.sum(axis=(0, 2)).reshape(1, 128, 1) / NT
    rs = 1.0 / np.sqrt(((X - mu) ** 2).sum(axis=(0, 2)).reshape(1, 128, 1) / NT + EPS)
    n = (X - mu) * rs
    DY = dy.astype(np.float64)
    a = DY.sum(axis=(0, 2)).reshape(1, 128, 1) / NT; c = (DY * n).sum(axis=(0, 2)).reshape(1, 128, 1) / NT
    return {"dx": (rs * (DY - a - n * c)).astype(np.float32)}

import math
from concourse.bass import DstId, RemoteDMATransfer
from concourse.mybir import AluOpType, AxisListType, ActivationFunctionType

TK = 512
H = TK // 2
EPS = 0.01

SCRATCH = {
    "xs": ("sbuf", [128, TK], "float32"),
    "dys": ("sbuf", [128, TK], "float32"),
    "j1": ("sbuf", [128, TK], "float32"),
    "j2": ("sbuf", [128, TK], "float32"),
    "j3": ("sbuf", [128, H], "float32"),
    "j4": ("sbuf", [128, 32], "float32"),
    "pr": ("sbuf", [128, TK], "float32"),
    "gx": ("sbuf", [128, 64], "float32"),
    "gd": ("sbuf", [128, 64], "float32"),
    "cv": ("sbuf", [128, 16], "float32"),
    "cs": ("sbuf", [128, 8], "float32"),
    "zb": ("sbuf", [128, TK], "float32"),
    "dxs": ("sbuf", [128, TK], "float32"),
    "xp": ("psum", [128, TK], "float32"),
    "tp": ("psum", [128, TK], "float32"),
}
SEMAPHORES = ["ldx", "ldy", "st", "pad", "vx", "sxq", "xpd", "p0", "p1", "vd", "sd3",
              "ax1", "ax2", "ad1", "ad2", "sent",
              "c_sx", "c_exe", "c_tmp", "c_mu", "c_v", "c_w", "c_sd", "c_rs", "c_na", "c_m", "c_k", "c_q",
              "c_t", "c_z0", "c_z1", "c_nars", "c_s0", "c_s1"]


def _bits(mask):
    return [b for b in range(16) if (mask >> b) & 1]


def rank_program(g, core, T, topo):
    if T.rank_of(core) is None:
        return
    cores = list(T.cores)
    n_ranks = len(cores)
    nt = n_ranks * TK
    S = T.sem
    V, A, Q = g.vector, g.scalar, g.sync
    ADD, SUB, MUL = AluOpType.add, AluOpType.subtract, AluOpType.mult
    X = AxisListType.X
    F = ActivationFunctionType

    def on_chip(a, b):
        return topo.host(a) == topo.host(b) and topo.chip(a) == topo.chip(b)

    def idx(c):
        return sorted(d for d in cores if on_chip(c, d)).index(c)

    def rk(c):
        return topo.rack(topo.host(c))

    def row_of(c):
        return sorted(d for d in cores if rk(d) == rk(c) and idx(d) // 2 == idx(c) // 2)

    def col_of(c):
        return sorted(d for d in cores if idx(d) % 2 == idx(c) % 2
                      and (on_chip(c, d) or (rk(d) != rk(c) and topo.may_write(c, d))))

    rows = sorted(set(tuple(row_of(c)) for c in cores))
    my_row = tuple(row_of(core))
    blk = rows.index(my_row) * 16
    o = blk + my_row.index(core) * 4

    def hop(buf, lo, hi, mates, sem):
        near = [d for d in mates if on_chip(core, d)]
        far = [d for d in mates if not on_chip(core, d)]
        far_mask = topo.mask(core, far[0])
        for d in far:
            far_mask &= topo.mask(core, d)
        near_mask = topo.mask(core, near[0]) & ~far_mask
        trs = []
        for ds, m in ((near, near_mask), (far, far_mask)):
            ids = []
            for d in ds:
                rid, pid = topo.addr(d, core)
                ids.append(DstId(rid=rid, pnc=pid))
            trs.append(RemoteDMATransfer(dst_ids=ids, dma_engine_mask=m, remote_sem=sem,
                                         srcs=[buf[:, lo:hi]], dsts=[buf[:, lo:hi] for _ in ds], alu_op=0))
        g.remote_dma_fused(trs, local_sem=S.sent)
        return len(_bits(near_mask)) + len(_bits(far_mask))

    def arrivals(mates):
        n = 0
        for d in mates:
            far_m = topo.mask(d, [e for e in cores if not on_chip(d, e) and topo.may_write(d, e)][0])
            n += len(_bits(topo.mask(d, core) & ~far_m)) if on_chip(d, core) else len(_bits(topo.mask(d, core)))
        return n

    row_mates = [d for d in my_row if d != core]
    col_mates = [d for d in col_of(core) if d != core]
    n_row, n_col = arrivals(row_mates), arrivals(col_mates)

    gx, gd, cv, cs = T.gx, T.gd, T.cv, T.cs
    c_sx, c_tmp, c_mu, c_v, c_w, c_na, c_m, c_k, c_q = (cv[:, i:i + 1] for i in range(9))
    c_exe, c_sd, c_rs, c_nars = (cs[:, i:i + 1] for i in range(4))

    Q.dma_start(T.xs[:], T.x[:]).then_inc(S.ldx, 16)
    Q.dma_start(T.dys[:], T.dy[:]).then_inc(S.ldy, 16)

    V.memset(gx[:, o + 2:o + 3], 0.0).then_inc(S.pad, 1)
    V.memset(gx[:, o + 3:o + 4], EPS / n_ranks).then_inc(S.pad, 1)
    V.wait_ge(S.ldx, 16)
    V.tensor_reduce(gx[:, o:o + 1], T.xs[:], X, ADD).then_inc(S.vx, 1)
    V.tensor_scalar(T.xp[:], T.xs[:], 1.0 / nt, None, MUL).then_inc(S.xpd, 1)
    V.wait_ge(S.xpd, 1)
    V.wait_ge(S.ldy, 16)
    V.tensor_tensor(T.pr[:, 0:H], T.xp[:, 0:H], T.dys[:, 0:H], MUL).then_inc(S.p0, 1)
    V.tensor_tensor(T.pr[:, H:TK], T.xp[:, H:TK], T.dys[:, H:TK], MUL).then_inc(S.p1, 1)
    V.wait_ge(S.p0, 1)
    V.tensor_reduce(gd[:, o + 1:o + 2], T.pr[:, 0:H], X, ADD).then_inc(S.vd, 1)

    A.wait_ge(S.ldx, 16)
    A.activation(T.j1[:], T.xs[:], F.Square, scale=1.0 / math.sqrt(nt), accum_out=gx[:, o + 1:o + 2]).then_inc(S.sxq, 1)
    A.wait_ge(S.ldy, 16)
    A.activation(T.j2[:, 0:H], T.dys[:, 0:H], F.Copy, scale=1.0 / nt, accum_out=gd[:, o:o + 1]).then_inc(S.sd3, 1)
    A.activation(T.j2[:, H:TK], T.dys[:, H:TK], F.Copy, scale=1.0 / nt, accum_out=gd[:, o + 2:o + 3]).then_inc(S.sd3, 1)
    A.wait_ge(S.p1, 1)
    A.activation(T.j3[:], T.pr[:, H:TK], F.Copy, accum_out=gd[:, o + 3:o + 4]).then_inc(S.sd3, 1)

    sent = 0
    g.wait_ge(S.pad, 2)
    g.wait_ge(S.vx, 1)
    g.wait_ge(S.sxq, 1)
    sent += hop(gx, o, o + 4, row_mates, S.ax1)
    g.wait_ge(S.vd, 1)
    g.wait_ge(S.sd3, 3)
    sent += hop(gd, o, o + 4, row_mates, S.ad1)
    g.wait_ge(S.ax1, n_row)
    sent += hop(gx, blk, blk + 16, col_mates, S.ax2)
    g.wait_ge(S.ad1, n_row)
    sent += hop(gd, blk, blk + 16, col_mates, S.ad2)
    g.wait_ge(S.sent, sent)
    g.wait_ge(S.ax2, n_col)
    g.wait_ge(S.ad2, n_col)

    for q_ in (V, A):
        q_.wait_ge(S.pad, 2)
        q_.wait_ge(S.vx, 1)
        q_.wait_ge(S.sxq, 1)
        q_.wait_ge(S.ax1, n_row)
        q_.wait_ge(S.ax2, n_col)
    V.tensor_reduce(c_sx, gx[:, 0:64:2], X, ADD).then_inc(S.c_sx, 1)
    A.activation(T.j4[:], gx[:, 1:64:2], F.Copy, accum_out=c_exe).then_inc(S.c_exe, 1)
    V.wait_ge(S.c_sx, 1)
    V.tensor_scalar(c_tmp, c_sx, c_sx, 1.0 / (float(nt) * float(nt)), MUL, MUL).then_inc(S.c_tmp, 1)
    A.wait_ge(S.c_exe, 1)
    A.wait_ge(S.c_tmp, 1)
    A.activation(c_sd, c_tmp, F.Sqrt, bias=c_exe, scale=-1.0).then_inc(S.c_sd, 1)
    V.wait_ge(S.c_tmp, 1)
    V.wait_ge(S.c_exe, 1)
    V.tensor_scalar(c_v, c_tmp, -1.0, c_exe, MUL, ADD).then_inc(S.c_v, 1)
    V.tensor_scalar(c_mu, c_sx, 1.0 / nt, None, MUL).then_inc(S.c_mu, 1)
    V.wait_ge(S.c_v, 1)
    V.reciprocal(c_w, c_v).then_inc(S.c_w, 1)
    A.wait_ge(S.c_sd, 1)
    A.wait_ge(S.c_w, 1)
    A.activation(c_rs, c_sd, F.Copy, scale=c_w).then_inc(S.c_rs, 1)

    V.wait_ge(S.vd, 1)
    V.wait_ge(S.sd3, 3)
    V.wait_ge(S.ad1, n_row)
    V.wait_ge(S.ad2, n_col)
    V.tensor_reduce(c_na, gd[:, 0:64:2], X, ADD, negate=True).then_inc(S.c_na, 1)
    V.tensor_reduce(c_m, gd[:, 1:64:2], X, ADD).then_inc(S.c_m, 1)
    V.wait_ge(S.c_na, 1)
    V.wait_ge(S.c_m, 1)
    V.wait_ge(S.c_mu, 1)
    V.tensor_scalar(c_k, c_na, c_mu, c_m, MUL, ADD).then_inc(S.c_k, 1)
    V.wait_ge(S.c_k, 1)
    V.wait_ge(S.c_w, 1)
    V.tensor_scalar(c_q, c_k, c_w, None, MUL).then_inc(S.c_q, 1)
    V.wait_ge(S.c_q, 1)
    V.tensor_scalar(T.tp[:], T.xs[:], c_mu, c_q, SUB, MUL).then_inc(S.c_t, 1)
    V.wait_ge(S.c_t, 1)
    V.tensor_tensor(T.zb[:, 0:H], T.dys[:, 0:H], T.tp[:, 0:H], SUB).then_inc(S.c_z0, 1)
    V.tensor_tensor(T.zb[:, H:TK], T.dys[:, H:TK], T.tp[:, H:TK], SUB).then_inc(S.c_z1, 1)
    A.wait_ge(S.c_rs, 1)
    A.wait_ge(S.c_na, 1)
    A.activation(c_nars, c_na, F.Copy, scale=c_rs).then_inc(S.c_nars, 1)
    A.wait_ge(S.c_nars, 1)
    A.wait_ge(S.c_z0, 1)
    A.activation(T.dxs[:, 0:H], T.zb[:, 0:H], F.Identity, bias=c_nars, scale=c_rs).then_inc(S.c_s0, 1)
    V.wait_ge(S.c_z1, 1)
    V.wait_ge(S.c_rs, 1)
    V.tensor_scalar(T.dxs[:, H:TK], T.zb[:, H:TK], c_na, c_rs, ADD, MUL).then_inc(S.c_s1, 1)

    Q.wait_ge(S.c_s0, 1)
    Q.wait_ge(S.c_s1, 1)
    Q.dma_start(T.dx[:], T.dxs[:]).then_inc(S.st, 16)
    Q.wait_ge(S.st, 16)
